import numpy as np
import ml_dtypes


def mxq(x, axis, fmt="e4m3"):
    dtype, down = {"e4m3": (ml_dtypes.float8_e4m3fn, 7), "e5m2": (ml_dtypes.float8_e5m2, 14)}[fmt]
    v = np.moveaxis(np.asarray(x, np.float32).astype(ml_dtypes.bfloat16).astype(np.float64), axis, -1)
    blocks = v.reshape(v.shape[:-1] + (-1, 32))
    amax = np.abs(blocks).max(-1, keepdims=True)
    byte = np.maximum(np.where(amax > 0, np.frexp(amax)[1] - 1 + 127, 0) - down, 1)
    scale = np.exp2(byte - 127.0)
    codes = (blocks / scale).astype(np.float32).astype(dtype).astype(np.float64)
    return np.moveaxis((codes * scale).reshape(v.shape), -1, axis)


WIDE = False


def mx_kscale(k):
    if not WIDE:
        return np.ones(k)
    levels = np.array([10, -10, 5, -5, 0])
    if k % 512:
        return np.exp2(np.random.permutation(np.resize(levels, k // 32))).repeat(32)
    a = np.empty((k // 512, 16))
    for p in range(k // 512):
        a[p, :8] = np.random.permutation(np.resize(levels, 8))
        for g in range(8):
            far = levels[np.abs(levels - a[p, g]) >= 10]
            a[p, g + 8] = far[np.random.randint(len(far))]
    return np.exp2(a.ravel()).repeat(32)


def f64(x):
    return np.asarray(x).astype(np.float64)


def striped(idx):
    return np.tile(idx.reshape(-1, 16).T, (8, 1)).astype(np.uint16)


def unstriped(offs):
    return offs[:16].T.reshape(-1).astype(np.int64)


E2M1 = np.array([0.0, 0.5, 1.0, 1.5, 2.0, 3.0, 4.0, 6.0, -0.0, -0.5, -1.0, -1.5, -2.0, -3.0, -4.0, -6.0])


def pack_fp4(w):
    k, n = w.shape
    w = f64(np.asarray(w, np.float32).astype(ml_dtypes.bfloat16)).reshape(k // 32, 32, n)
    amax = np.abs(w).max(1)
    mant, ex = np.frexp(amax / 6.0)
    byte = np.clip(np.where(amax > 0, np.where(mant > 0.5, ex, ex - 1) + 127, 1), 1, 254)
    scaled = (w * np.exp2(127.0 - byte)[:, None, :]).reshape(k, n).astype(np.float32)
    c = np.ascontiguousarray(scaled.reshape(k // 512, 128, 4, n).transpose(0, 1, 3, 2)).astype(ml_dtypes.float4_e2m1fn).view(np.uint8) & 0xF
    words = (c[..., 0::2] | (c[..., 1::2] << 4)).reshape(k // 512, 128, 2 * n)
    return np.ascontiguousarray(words), np.ascontiguousarray(byte.astype(np.uint8).reshape(k // 512, 16, n))


def unpack_fp4(words, scales):
    g, _, n = scales.shape
    words = np.ascontiguousarray(words).reshape(g, 128, n, 2)
    nib = np.empty((g, 128, n, 4), np.uint8)
    nib[..., 0::2] = words & 0xF
    nib[..., 1::2] = words >> 4
    vals = E2M1[nib] * np.repeat(np.exp2(scales.astype(np.float64) - 127.0), 8, axis=1)[..., None]
    return vals.transpose(0, 1, 3, 2).reshape(g * 512, n)


def silu(v):
    return v / (1.0 + np.exp(-np.maximum(v, -700.0)))


K, T, N = 1024, 512, 128


def setup_inputs():
    n = np.random.standard_normal
    s = mx_kscale(K)[:, None]
    packed_xT = pack_fp4(n((K, T)) * s)
    return {
        "x_words": packed_xT[0],
        "x_scales": packed_xT[1],
        "w1": (n((K, N)) / np.sqrt(K) / s).astype(np.float32),
        "w2": (n((K, N)) / np.sqrt(K) / s).astype(np.float32),
        "w3": (n((K, N)) / np.sqrt(K) / s).astype(np.float32),
        "pos1": striped(np.random.permutation(T)),
        "pos2": striped(np.random.permutation(T)),
        "pos3": striped(np.random.permutation(T)),
    }


def reference(x_words, x_scales, w1, w2, w3, pos1, pos2, pos3):
    xq = unpack_fp4(x_words, x_scales)
    h = mxq(f64(w3), 0, "e4m3").T @ xq
    g = mxq(f64(w1), 0, "e4m3").T @ xq
    s = mxq(f64(w2), 0, "e4m3").T @ xq
    return silu(h[:, unstriped(pos1)] * g + s) + silu(h[:, unstriped(pos2)] * g + s) + silu(h[:, unstriped(pos3)] * g + s)

@@ -1,0 +1,217 @@
+from contextlib import ExitStack
+
+import concourse.mybir as mybir
+from concourse.masks import make_identity
+
+K, T, M = 1024, 512, 128
+FLOPS = 3 * 2 * K * T * M
+
+F32 = mybir.dt.float32
+BF16 = mybir.dt.bfloat16
+I32 = mybir.dt.int32
+U32 = mybir.dt.uint32
+U16 = mybir.dt.uint16
+U8 = mybir.dt.uint8
+FP8X4 = mybir.dt.float8_e4m3fn_x4
+FP4X4 = mybir.dt.float4_e2m1fn_x4
+MULT = mybir.AluOpType.mult
+ADD = mybir.AluOpType.add
+SILU = mybir.ActivationFunctionType.Silu
+
+P = 128
+PACK = 4
+K_PASS = P * PACK
+PASSES = K // K_PASS
+D = 3
+CH = 128
+CHUNKS = T // CH
+LIST_COLS = CH // 16
+SPLIT = 88
+
+
+def tile_picked_wfilmg_silu_l_kernel(tc, x_words, x_scales, w1, w2, w3, pos1, pos2, pos3, out):
+    nc = tc.nc
+    with ExitStack() as ctx:
+        sb = ctx.enter_context(tc.tile_pool(name="sb", bufs=1))
+        ps = ctx.enter_context(tc.psum_pool(name="ps", bufs=1))
+
+        lists = [sb.tile([P, T // 16], U16, name=f"list{d}") for d in range(D)]
+        xw = [sb.tile([P, 2 * T], U8, name=f"xw{z}", align_bytes=64) for z in range(PASSES)]
+        xs = sb.tile([P, PASSES, T], U8, align_bytes=64)
+        raw_h = sb.tile([P, PASSES, PACK, M], F32)
+        raw_g = sb.tile([P, PASSES, PACK, M], F32)
+        raw_s = [sb.tile([P, PACK, M], F32, name=f"raw_s{z}", tag=f"raw_s{z}") for z in range(PASSES)]
+        grp_h = sb.tile([P, PASSES, M * PACK], BF16, align_bytes=64)
+        grp_g = sb.tile([P, PASSES, M * PACK], BF16, align_bytes=64)
+        grp_s = [sb.tile([P, M * PACK], BF16, name=f"grp_s{z}", tag=f"grp_s{z}", align_bytes=64) for z in range(PASSES)]
+        grouped = {}
+        codes, scales = {}, {}
+        for z in range(PASSES):
+            grouped["h", z], grouped["g", z], grouped["s", z] = grp_h[:, z], grp_g[:, z], grp_s[z][:]
+            for n in "hgs":
+                codes[n, z] = sb.tile([P, M], U32, name=f"codes_{n}{z}", align_bytes=64)
+                scales[n, z] = sb.tile([P, M], U8, name=f"scales_{n}{z}", align_bytes=64)
+
+        def load_whole(dst, w):
+            nc.sync.dma_start(out=dst[:], in_=w.rearrange("(z p j) m -> p z j m", z=PASSES, j=PACK))
+
+        def load_s(z):
+            rows = w2[z * K_PASS : (z + 1) * K_PASS, :]
+            nc.sync.dma_start(out=raw_s[z][:], in_=rows.rearrange("(p j) m -> p j m", j=PACK))
+
+        def load_x(z):
+            nc.sync.dma_start(out=xw[z][:].bitcast(I32), in_=x_words[z].bitcast(I32))
+
+        def cast_whole(grp, raw):
+            dst = grp[:].rearrange("p z (c i t) -> p z c t i", i=4, t=PACK)
+            src = raw[:].rearrange("p z t (c i) -> p z c t i", i=4)
+            nc.vector.tensor_copy(out=dst[:, :, : SPLIT // 4], in_=src[:, :, : SPLIT // 4])
+            nc.scalar.copy(out=dst[:, :, SPLIT // 4 :], in_=src[:, :, SPLIT // 4 :])
+
+        def cast_s(z, copy):
+            dst = grp_s[z][:].rearrange("p (c i t) -> p c t i", i=4, t=PACK)
+            copy(out=dst, in_=raw_s[z][:].rearrange("p t (c i) -> p c t i", i=4))
+
+        def quant(n, z):
+            nc.vector.quantize_mx(out=codes[n, z][:].bitcast(FP8X4), scales=scales[n, z][:], in_=grouped[n, z])
+
+        def mm(dst, n, z, c0, c1):
+            nc.tensor.matmul_mx(
+                out=dst,
+                lhsT=codes[n, z][:].bitcast(FP8X4),
+                lhsT_scale=scales[n, z][:],
+                rhs=xw[z][:, 2 * c0 : 2 * c1].bitcast(FP4X4),
+                rhs_scale=xs[:, z, c0:c1],
+                start=(z == 0),
+                stop=(z == PASSES - 1),
+            )
+
+        def mm_chunks(n, first, rest):
+            for c in range(CHUNKS):
+                bank = first if c == 0 else rest
+                for z in range(PASSES):
+                    mm(bank[:, c * CH : (c + 1) * CH], n, z, c * CH, (c + 1) * CH)
+
+        nc.vector.memset(xs[:].rearrange("p z t -> p (z t)").bitcast(I32), 0)
+        zero_in = sb.tile([P, 1], F32)
+        zero = sb.tile([P, 1], F32)
+        nc.vector.memset(zero_in[:], 0.0)
+
+        load_whole(raw_h, w3)
+        for q in range(4):
+            nc.sync.dma_start(
+                out=xs[32 * q : 32 * q + 4, :, :].bitcast(I32),
+                in_=x_scales[:, 4 * q : 4 * q + 4, :].rearrange("z r t -> r z t").bitcast(I32),
+            )
+        load_x(0)
+        load_whole(raw_g, w1)
+        load_x(1)
+        load_s(0)
+        nc.sync.dma_start(lists[0][:], pos1)
+        load_s(1)
+        nc.sync.dma_start(lists[1][:], pos2)
+        nc.sync.dma_start(lists[2][:], pos3)
+
+        nc.scalar.activation(out=zero[:], in_=zero_in[:], func=SILU)
+        ident = sb.tile([P, P], F32)
+        make_identity(nc, ident[:])
+
+        h_ps = ps.tile([P, T], F32, tag="b0", name="h_ps")
+        g0_ps = ps.tile([P, T], F32, tag="b1", name="g0_ps")
+        gr_ps = ps.tile([P, T], F32, tag="b2", name="gr_ps")
+        s0_ps = ps.tile([P, T], F32, tag="b3", name="s0_ps")
+        sr_ps = ps.tile([P, T], F32, tag="b4", name="sr_ps")
+        h_sb = sb.tile([P, T], F32)
+
+        cast_whole(grp_h, raw_h)
+        quant("h", 0)
+        mm(h_ps[:], "h", 0, 0, T)
+        quant("h", 1)
+        cast_whole(grp_g, raw_g)
+        mm(h_ps[:], "h", 1, 0, T)
+        quant("g", 0)
+        quant("g", 1)
+        nc.scalar.copy(out=h_sb[:], in_=h_ps[:])
+        mm_chunks("g", g0_ps, gr_ps)
+        cast_s(0, nc.vector.tensor_copy)
+        g0_sb = sb.tile([P, CH], F32, tag="raw_s0")
+        nc.vector.tensor_copy(out=g0_sb[:], in_=g0_ps[:, :CH])
+        cast_s(1, nc.scalar.copy)
+        gr_sb = sb.tile([P, T - CH], F32, tag="raw_s1")
+        nc.scalar.copy(out=gr_sb[:], in_=gr_ps[:, CH:])
+
+        t = {}
+
+        def gather(c, d, tag=""):
+            t[c, d] = sb.tile([P, CH], F32, name=f"t{c}_{d}", tag=tag, align_bytes=64)
+            nc.vector.tensor_tensor(
+                t[c, d][:],
+                h_sb[:].indirect(lists[d][:, c * LIST_COLS : (c + 1) * LIST_COLS]),
+                g0_sb[:] if c == 0 else gr_sb[:, (c - 1) * CH : c * CH],
+                MULT,
+            )
+
+        gather(0, 0)
+        quant("s", 0)
+        gather(0, 1, "grp_s0")
+        quant("s", 1)
+        gather(0, 2, "grp_s1")
+        mm_chunks("s", s0_ps, sr_ps)
+        s0_sb = sb.tile([P, CH], F32)
+        sr_sb = sb.tile([P, T - 2 * CH], F32)
+        nc.scalar.copy(out=s0_sb[:], in_=s0_ps[:, :CH])
+        nc.scalar.copy(out=sr_sb[:], in_=sr_ps[:, CH : T - CH])
+
+        def xpose(dst, src, start, stop):
+            nc.tensor.matmul(dst, lhsT=src, rhs=ident[:], start=start, stop=stop, is_transpose=True)
+
+        u_tags = ("b5", "b6", "b0")
+        o_tags = ("b7", "b1", "b2")
+        y = {}
+
+        def forward(c):
+            u_ps = ps.tile([P, T], F32, tag=u_tags[c], name=f"u_ps{c}")
+            s_c = s0_sb[:] if c == 0 else sr_sb[:, (c - 1) * CH : c * CH]
+            for d in range(D):
+                dst = u_ps[:, d * P : (d + 1) * P]
+                xpose(dst, s_c, True, False)
+                xpose(dst, t[c, d][:], False, True)
+            y[c] = sb.tile([P, D * P], F32, name=f"y{c}")
+            nc.scalar.activation(out=y[c][:], in_=u_ps[:, : D * P], func=SILU, bias=zero[:])
+
+        def back(c):
+            o_ps = ps.tile([P, T], F32, tag=o_tags[c], name=f"o_ps{c}")
+            for d in range(D):
+                xpose(o_ps[:, :CH], y[c][:, d * P : (d + 1) * P], d == 0, d == D - 1)
+            o_sb = sb.tile([P, CH], F32, name=f"o_sb{c}")
+            nc.scalar.copy(out=o_sb[:], in_=o_ps[:, :CH])
+            nc.sync.dma_start(out=out[:, c * CH : (c + 1) * CH], in_=o_sb[:])
+
+        forward(0)
+        for c in range(1, CHUNKS - 1):
+            for d in range(D):
+                gather(c, d)
+            forward(c)
+            back(c - 1)
+
+        c = CHUNKS - 1
+        cols = slice(c * CH, (c + 1) * CH)
+        u = [t[1, 2], t[2, 1], t[2, 2]]
+        yl = [sb.tile([P, CH], F32, name=f"yl{d}") for d in range(D)]
+
+        def shift(d):
+            nc.vector.tensor_tensor(u[d][:], t[c, d][:], sr_ps[:, cols], ADD)
+            nc.scalar.activation(out=yl[d][:], in_=u[d][:], func=SILU, bias=zero[:])
+
+        gather(c, 0)
+        gather(c, 1)
+        shift(0)
+        back(c - 1)
+        gather(c, 2)
+        shift(1)
+        shift(2)
+        part = sb.tile([P, CH], F32)
+        o_last = sb.tile([P, CH], F32)
+        nc.vector.tensor_tensor(part[:], yl[0][:], yl[1][:], ADD)
+        nc.vector.tensor_tensor(o_last[:], part[:], yl[2][:], ADD)
+        nc.sync.dma_start(out=out[:, cols], in_=o_last[:])

@@ -26,6 +26,7 @@ D = 3
 CH = 128
 CHUNKS = T // CH
 LIST_COLS = CH // 16
+WIDE = 160
 SPLIT = 88
 
 
@@ -36,18 +37,18 @@ def tile_picked_wfilmg_silu_l_kernel(tc, x_words, x_scales, w1, w2, w3, pos1, po
         ps = ctx.enter_context(tc.psum_pool(name="ps", bufs=1))
 
         lists = [sb.tile([P, T // 16], U16, name=f"list{d}") for d in range(D)]
-        xw = [sb.tile([P, 2 * T], U8, name=f"xw{z}", align_bytes=64) for z in range(PASSES)]
+        xw = sb.tile([P, PASSES, 2 * T], U8, align_bytes=64)
         xs = sb.tile([P, PASSES, T], U8, align_bytes=64)
         raw_h = sb.tile([P, PASSES, PACK, M], F32)
-        raw_g = sb.tile([P, PASSES, PACK, M], F32)
+        raw_g = [sb.tile([P, PACK, M], F32, name=f"raw_g{z}", tag=f"raw_g{z}") for z in range(PASSES)]
         raw_s = [sb.tile([P, PACK, M], F32, name=f"raw_s{z}", tag=f"raw_s{z}") for z in range(PASSES)]
         grp_h = sb.tile([P, PASSES, M * PACK], BF16, align_bytes=64)
-        grp_g = sb.tile([P, PASSES, M * PACK], BF16, align_bytes=64)
+        grp_g = [sb.tile([P, M * PACK], BF16, name=f"grp_g{z}", align_bytes=64) for z in range(PASSES)]
         grp_s = [sb.tile([P, M * PACK], BF16, name=f"grp_s{z}", tag=f"grp_s{z}", align_bytes=64) for z in range(PASSES)]
         grouped = {}
         codes, scales = {}, {}
         for z in range(PASSES):
-            grouped["h", z], grouped["g", z], grouped["s", z] = grp_h[:, z], grp_g[:, z], grp_s[z][:]
+            grouped["h", z], grouped["g", z], grouped["s", z] = grp_h[:, z], grp_g[z][:], grp_s[z][:]
             for n in "hgs":
                 codes[n, z] = sb.tile([P, M], U32, name=f"codes_{n}{z}", align_bytes=64)
                 scales[n, z] = sb.tile([P, M], U8, name=f"scales_{n}{z}", align_bytes=64)
@@ -55,22 +56,14 @@ def tile_picked_wfilmg_silu_l_kernel(tc, x_words, x_scales, w1, w2, w3, pos1, po
         def load_whole(dst, w):
             nc.sync.dma_start(out=dst[:], in_=w.rearrange("(z p j) m -> p z j m", z=PASSES, j=PACK))
 
-        def load_s(z):
-            rows = w2[z * K_PASS : (z + 1) * K_PASS, :]
-            nc.sync.dma_start(out=raw_s[z][:], in_=rows.rearrange("(p j) m -> p j m", j=PACK))
+        def load_pass(dst, w, z):
+            rows = w[z * K_PASS : (z + 1) * K_PASS, :]
+            nc.sync.dma_start(out=dst[z][:], in_=rows.rearrange("(p j) m -> p j m", j=PACK))
 
-        def load_x(z):
-            nc.sync.dma_start(out=xw[z][:].bitcast(I32), in_=x_words[z].bitcast(I32))
-
-        def cast_whole(grp, raw):
-            dst = grp[:].rearrange("p z (c i t) -> p z c t i", i=4, t=PACK)
-            src = raw[:].rearrange("p z t (c i) -> p z c t i", i=4)
-            nc.vector.tensor_copy(out=dst[:, :, : SPLIT // 4], in_=src[:, :, : SPLIT // 4])
-            nc.scalar.copy(out=dst[:, :, SPLIT // 4 :], in_=src[:, :, SPLIT // 4 :])
-
-        def cast_s(z, copy):
-            dst = grp_s[z][:].rearrange("p (c i t) -> p c t i", i=4, t=PACK)
-            copy(out=dst, in_=raw_s[z][:].rearrange("p t (c i) -> p c t i", i=4))
+        def cast_pass(grp, raw, copy, m0=0, m1=M):
+            dst = grp.rearrange("p (c i t) -> p c t i", i=4, t=PACK)
+            src = raw.rearrange("p t (c i) -> p c t i", i=4)
+            copy(out=dst[:, m0 // 4 : m1 // 4], in_=src[:, m0 // 4 : m1 // 4])
 
         def quant(n, z):
             nc.vector.quantize_mx(out=codes[n, z][:].bitcast(FP8X4), scales=scales[n, z][:], in_=grouped[n, z])
@@ -80,22 +73,26 @@ def tile_picked_wfilmg_silu_l_kernel(tc, x_words, x_scales, w1, w2, w3, pos1, po
                 out=dst,
                 lhsT=codes[n, z][:].bitcast(FP8X4),
                 lhsT_scale=scales[n, z][:],
-                rhs=xw[z][:, 2 * c0 : 2 * c1].bitcast(FP4X4),
+                rhs=xw[:, z, 2 * c0 : 2 * c1].bitcast(FP4X4),
                 rhs_scale=xs[:, z, c0:c1],
                 start=(z == 0),
                 stop=(z == PASSES - 1),
             )
 
-        def mm_chunks(n, first, rest):
+        def mm_chunks(n, banks):
             for c in range(CHUNKS):
-                bank = first if c == 0 else rest
+                bank = banks[min(c, len(banks) - 1)]
                 for z in range(PASSES):
                     mm(bank[:, c * CH : (c + 1) * CH], n, z, c * CH, (c + 1) * CH)
 
         nc.vector.memset(xs[:].rearrange("p z t -> p (z t)").bitcast(I32), 0)
         zero_in = sb.tile([P, 1], F32)
-        zero = sb.tile([P, 1], F32)
+        y_wide = sb.tile([P, D, WIDE], F32)
+        y_b = sb.tile([P, D, T - 2 * CH - WIDE], F32)
+        zero_tile = sb.tile([P, 1], F32)
+        zero = zero_tile[:]
         nc.vector.memset(zero_in[:], 0.0)
+        nc.vector.memset(y_wide[:, 0, 0:1], 0.0)
 
         load_whole(raw_h, w3)
         for q in range(4):
@@ -103,115 +100,132 @@ def tile_picked_wfilmg_silu_l_kernel(tc, x_words, x_scales, w1, w2, w3, pos1, po
                 out=xs[32 * q : 32 * q + 4, :, :].bitcast(I32),
                 in_=x_scales[:, 4 * q : 4 * q + 4, :].rearrange("z r t -> r z t").bitcast(I32),
             )
-        load_x(0)
-        load_whole(raw_g, w1)
-        load_x(1)
-        load_s(0)
+        nc.sync.dma_start(out=xw[:].bitcast(I32), in_=x_words.rearrange("z p b -> p z b").bitcast(I32))
+        load_pass(raw_g, w1, 0)
+        load_pass(raw_g, w1, 1)
+        load_pass(raw_s, w2, 0)
         nc.sync.dma_start(lists[0][:], pos1)
-        load_s(1)
+        load_pass(raw_s, w2, 1)
         nc.sync.dma_start(lists[1][:], pos2)
         nc.sync.dma_start(lists[2][:], pos3)
 
-        nc.scalar.activation(out=zero[:], in_=zero_in[:], func=SILU)
+        nc.scalar.activation(out=zero, in_=zero_in[:], func=SILU)
         ident = sb.tile([P, P], F32)
         make_identity(nc, ident[:])
 
         h_ps = ps.tile([P, T], F32, tag="b0", name="h_ps")
+        h2_ps = ps.tile([P, T], F32, tag="b6", name="h2_ps")
         g0_ps = ps.tile([P, T], F32, tag="b1", name="g0_ps")
         gr_ps = ps.tile([P, T], F32, tag="b2", name="gr_ps")
         s0_ps = ps.tile([P, T], F32, tag="b3", name="s0_ps")
+        s1_ps = ps.tile([P, T], F32, tag="b7", name="s1_ps")
         sr_ps = ps.tile([P, T], F32, tag="b4", name="sr_ps")
-        h_sb = sb.tile([P, T], F32)
 
-        cast_whole(grp_h, raw_h)
+        for z in range(PASSES):
+            cast_pass(grp_h[:, z], raw_h[:, z], nc.vector.tensor_copy, 0, SPLIT)
+            cast_pass(grp_h[:, z], raw_h[:, z], nc.scalar.copy, SPLIT, M)
         quant("h", 0)
-        mm(h_ps[:], "h", 0, 0, T)
         quant("h", 1)
-        cast_whole(grp_g, raw_g)
-        mm(h_ps[:], "h", 1, 0, T)
+        mm_chunks("h", (h_ps, h_ps, h2_ps))
+        cast_pass(grp_g[0][:], raw_g[0][:], nc.vector.tensor_copy)
         quant("g", 0)
+        cast_pass(grp_g[1][:], raw_g[1][:], nc.vector.tensor_copy, 0, SPLIT)
+        cast_pass(grp_g[1][:], raw_g[1][:], nc.scalar.copy, SPLIT, M)
         quant("g", 1)
-        nc.scalar.copy(out=h_sb[:], in_=h_ps[:])
-        mm_chunks("g", g0_ps, gr_ps)
-        cast_s(0, nc.vector.tensor_copy)
-        g0_sb = sb.tile([P, CH], F32, tag="raw_s0")
-        nc.vector.tensor_copy(out=g0_sb[:], in_=g0_ps[:, :CH])
-        cast_s(1, nc.scalar.copy)
+        h_sb = sb.tile([P, T], F32, tag="raw_g1")
+        nc.scalar.copy(out=h_sb[:, : T // 2], in_=h_ps[:, : T // 2])
+        nc.scalar.copy(out=h_sb[:, T // 2 :], in_=h2_ps[:, T // 2 :])
+        mm_chunks("g", (g0_ps, gr_ps))
+        cast_pass(grp_s[0][:], raw_s[0][:], nc.vector.tensor_copy)
+        quant("s", 0)
+        g0_sb = sb.tile([P, CH], F32)
+        nc.scalar.copy(out=g0_sb[:], in_=g0_ps[:, :CH])
+        cast_pass(grp_s[1][:], raw_s[1][:], nc.scalar.copy)
         gr_sb = sb.tile([P, T - CH], F32, tag="raw_s1")
         nc.scalar.copy(out=gr_sb[:], in_=gr_ps[:, CH:])
 
-        t = {}
-
-        def gather(c, d, tag=""):
-            t[c, d] = sb.tile([P, CH], F32, name=f"t{c}_{d}", tag=tag, align_bytes=64)
+        def gather(dst, d, c0, c1):
             nc.vector.tensor_tensor(
-                t[c, d][:],
-                h_sb[:].indirect(lists[d][:, c * LIST_COLS : (c + 1) * LIST_COLS]),
-                g0_sb[:] if c == 0 else gr_sb[:, (c - 1) * CH : c * CH],
+                dst,
+                h_sb[:].indirect(lists[d][:, c0 // 16 : c1 // 16]),
+                g0_sb[:] if c0 == 0 else gr_sb[:, c0 - CH : c1 - CH],
                 MULT,
             )
 
-        gather(0, 0)
-        quant("s", 0)
-        gather(0, 1, "grp_s0")
+        t = {}
+
+        def gather_block(c, d, tag=""):
+            t[c, d] = sb.tile([P, CH], F32, name=f"t{c}_{d}", tag=tag, align_bytes=64)
+            gather(t[c, d][:], d, c * CH, (c + 1) * CH)
+
+        gather_block(0, 0, "grp_s0")
+        gather_block(0, 1)
+        gather_block(0, 2)
         quant("s", 1)
-        gather(0, 2, "grp_s1")
-        mm_chunks("s", s0_ps, sr_ps)
+        mm_chunks("s", (s0_ps, s1_ps, sr_ps))
         s0_sb = sb.tile([P, CH], F32)
-        sr_sb = sb.tile([P, T - 2 * CH], F32)
+        sr_sb = sb.tile([P, CH], F32)
         nc.scalar.copy(out=s0_sb[:], in_=s0_ps[:, :CH])
-        nc.scalar.copy(out=sr_sb[:], in_=sr_ps[:, CH : T - CH])
+        nc.scalar.copy(out=sr_sb[:], in_=s1_ps[:, CH : 2 * CH])
 
         def xpose(dst, src, start, stop):
             nc.tensor.matmul(dst, lhsT=src, rhs=ident[:], start=start, stop=stop, is_transpose=True)
 
-        u_tags = ("b5", "b6", "b0")
-        o_tags = ("b7", "b1", "b2")
+        u_tags = ("b5", "b1")
+        o_tags = ("b0", "b6")
         y = {}
 
         def forward(c):
             u_ps = ps.tile([P, T], F32, tag=u_tags[c], name=f"u_ps{c}")
-            s_c = s0_sb[:] if c == 0 else sr_sb[:, (c - 1) * CH : c * CH]
+            s_c = s0_sb[:] if c == 0 else sr_sb[:]
             for d in range(D):
                 dst = u_ps[:, d * P : (d + 1) * P]
                 xpose(dst, s_c, True, False)
                 xpose(dst, t[c, d][:], False, True)
-            y[c] = sb.tile([P, D * P], F32, name=f"y{c}")
-            nc.scalar.activation(out=y[c][:], in_=u_ps[:, : D * P], func=SILU, bias=zero[:])
+            y[c] = sb.tile([P, D * P], F32, name=f"y{c}", tag=f"y{c}")
+            nc.scalar.activation(out=y[c][:], in_=u_ps[:, : D * P], func=SILU, bias=zero if c == 0 else y_wide[:, 0, 0:1])
 
-        def back(c):
+        def back(c, copy):
             o_ps = ps.tile([P, T], F32, tag=o_tags[c], name=f"o_ps{c}")
             for d in range(D):
                 xpose(o_ps[:, :CH], y[c][:, d * P : (d + 1) * P], d == 0, d == D - 1)
             o_sb = sb.tile([P, CH], F32, name=f"o_sb{c}")
-            nc.scalar.copy(out=o_sb[:], in_=o_ps[:, :CH])
+            copy(out=o_sb[:], in_=o_ps[:, :CH])
             nc.sync.dma_start(out=out[:, c * CH : (c + 1) * CH], in_=o_sb[:])
 
         forward(0)
-        for c in range(1, CHUNKS - 1):
-            for d in range(D):
-                gather(c, d)
-            forward(c)
-            back(c - 1)
+        for d in range(D):
+            gather_block(1, d, ("grp_s1", "", "t_late")[d])
+        forward(1)
+        back(0, nc.scalar.copy)
 
-        c = CHUNKS - 1
-        cols = slice(c * CH, (c + 1) * CH)
-        u = [t[1, 2], t[2, 1], t[2, 2]]
-        yl = [sb.tile([P, CH], F32, name=f"yl{d}") for d in range(D)]
+        a0, b0 = 2 * CH, 2 * CH + WIDE
+        nb = T - b0
+        t_a = sb.tile([P, D, WIDE], F32, tag="t_a")
+        u_a = sb.tile([P, D, WIDE], F32)
+        for d in range(D):
+            gather(t_a[:, d, :], d, a0, b0)
+        t_b = sb.tile([P, D - 1, nb], F32, tag="t_b")
+        for d in range(D - 1):
+            gather(t_b[:, d, :], d, b0, T)
+        nc.vector.tensor_tensor(u_a[:], t_a[:], sr_ps[:, a0:b0].unsqueeze(1).to_broadcast([P, D, WIDE]), ADD)
+        nc.scalar.activation(out=y_wide[:], in_=u_a[:], func=SILU, bias=zero)
 
-        def shift(d):
-            nc.vector.tensor_tensor(u[d][:], t[c, d][:], sr_ps[:, cols], ADD)
-            nc.scalar.activation(out=yl[d][:], in_=u[d][:], func=SILU, bias=zero[:])
+        t_last = sb.tile([P, nb], F32, tag="t_late", align_bytes=64)
+        gather(t_last[:], D - 1, b0, T)
+        u_b = sb.tile([P, D, nb], F32, tag="y0")
+        nc.vector.tensor_tensor(u_b[:, : D - 1], t_b[:], sr_ps[:, b0:].unsqueeze(1).to_broadcast([P, D - 1, nb]), ADD)
+        nc.scalar.activation(out=y_b[:, : D - 1, :], in_=u_b[:, : D - 1], func=SILU, bias=zero)
+        nc.vector.tensor_tensor(u_b[:, D - 1], t_last[:], sr_ps[:, b0:], ADD)
+        nc.scalar.activation(out=y_b[:, D - 1, :], in_=u_b[:, D - 1], func=SILU, bias=zero)
 
-        gather(c, 0)
-        gather(c, 1)
-        shift(0)
-        back(c - 1)
-        gather(c, 2)
-        shift(1)
-        shift(2)
-        part = sb.tile([P, CH], F32)
-        o_last = sb.tile([P, CH], F32)
-        nc.vector.tensor_tensor(part[:], yl[0][:], yl[1][:], ADD)
-        nc.vector.tensor_tensor(o_last[:], part[:], yl[2][:], ADD)
-        nc.sync.dma_start(out=out[:, cols], in_=o_last[:])
+        part = sb.tile([P, T - a0], F32)
+        o_a = u_b[:, : D - 1].rearrange("p d n -> p (d n)")[:, :WIDE]
+        o_b = sb.tile([P, nb], F32)
+        nc.vector.tensor_tensor(part[:, :WIDE], y_wide[:, 0, :], y_wide[:, 1, :], ADD)
+        nc.vector.tensor_tensor(part[:, WIDE:], y_b[:, 0, :], y_b[:, 1, :], ADD)
+        nc.vector.tensor_tensor(o_a[:], part[:, :WIDE], y_wide[:, 2, :], ADD)
+        nc.sync.dma_start(out=out[:, a0:b0], in_=o_a[:])
+        nc.vector.tensor_tensor(o_b[:], part[:, WIDE:], y_b[:, 2, :], ADD)
+        nc.sync.dma_start(out=out[:, b0:], in_=o_b[:])
+        back(1, nc.scalar.copy)

from contextlib import ExitStack

import concourse.mybir as mybir
from concourse.masks import make_identity

K, T, M = 1024, 512, 128
FLOPS = 3 * 2 * K * T * M

F32 = mybir.dt.float32
BF16 = mybir.dt.bfloat16
I32 = mybir.dt.int32
U32 = mybir.dt.uint32
U16 = mybir.dt.uint16
U8 = mybir.dt.uint8
FP8X4 = mybir.dt.float8_e4m3fn_x4
FP4X4 = mybir.dt.float4_e2m1fn_x4
MULT = mybir.AluOpType.mult
ADD = mybir.AluOpType.add
SILU = mybir.ActivationFunctionType.Silu

P = 128
PACK = 4
K_PASS = P * PACK
PASSES = K // K_PASS
D = 3
CH = 128
CHUNKS = T // CH
LIST_COLS = CH // 16
WIDE = 160
SPLIT = 88


def tile_picked_wfilmg_silu_l_kernel(tc, x_words, x_scales, w1, w2, w3, pos1, pos2, pos3, out):
    nc = tc.nc
    with ExitStack() as ctx:
        sb = ctx.enter_context(tc.tile_pool(name="sb", bufs=1))
        ps = ctx.enter_context(tc.psum_pool(name="ps", bufs=1))

        lists = [sb.tile([P, T // 16], U16, name=f"list{d}") for d in range(D)]
        xw = sb.tile([P, PASSES, 2 * T], U8, align_bytes=64)
        xs = sb.tile([P, PASSES, T], U8, align_bytes=64)
        raw_h = sb.tile([P, PASSES, PACK, M], F32)
        raw_g = [sb.tile([P, PACK, M], F32, name=f"raw_g{z}", tag=f"raw_g{z}") for z in range(PASSES)]
        raw_s = [sb.tile([P, PACK, M], F32, name=f"raw_s{z}", tag=f"raw_s{z}") for z in range(PASSES)]
        grp_h = sb.tile([P, PASSES, M * PACK], BF16, align_bytes=64)
        grp_g = [sb.tile([P, M * PACK], BF16, name=f"grp_g{z}", align_bytes=64) for z in range(PASSES)]
        grp_s = [sb.tile([P, M * PACK], BF16, name=f"grp_s{z}", tag=f"grp_s{z}", align_bytes=64) for z in range(PASSES)]
        grouped = {}
        codes, scales = {}, {}
        for z in range(PASSES):
            grouped["h", z], grouped["g", z], grouped["s", z] = grp_h[:, z], grp_g[z][:], grp_s[z][:]
            for n in "hgs":
                codes[n, z] = sb.tile([P, M], U32, name=f"codes_{n}{z}", align_bytes=64)
                scales[n, z] = sb.tile([P, M], U8, name=f"scales_{n}{z}", align_bytes=64)

        def load_whole(dst, w):
            nc.sync.dma_start(out=dst[:], in_=w.rearrange("(z p j) m -> p z j m", z=PASSES, j=PACK))

        def load_pass(dst, w, z):
            rows = w[z * K_PASS : (z + 1) * K_PASS, :]
            nc.sync.dma_start(out=dst[z][:], in_=rows.rearrange("(p j) m -> p j m", j=PACK))

        def cast_pass(grp, raw, copy, m0=0, m1=M):
            dst = grp.rearrange("p (c i t) -> p c t i", i=4, t=PACK)
            src = raw.rearrange("p t (c i) -> p c t i", i=4)
            copy(out=dst[:, m0 // 4 : m1 // 4], in_=src[:, m0 // 4 : m1 // 4])

        def quant(n, z):
            nc.vector.quantize_mx(out=codes[n, z][:].bitcast(FP8X4), scales=scales[n, z][:], in_=grouped[n, z])

        def mm(dst, n, z, c0, c1):
            nc.tensor.matmul_mx(
                out=dst,
                lhsT=codes[n, z][:].bitcast(FP8X4),
                lhsT_scale=scales[n, z][:],
                rhs=xw[:, z, 2 * c0 : 2 * c1].bitcast(FP4X4),
                rhs_scale=xs[:, z, c0:c1],
                start=(z == 0),
                stop=(z == PASSES - 1),
            )

        def mm_chunks(n, banks):
            for c in range(CHUNKS):
                bank = banks[min(c, len(banks) - 1)]
                for z in range(PASSES):
                    mm(bank[:, c * CH : (c + 1) * CH], n, z, c * CH, (c + 1) * CH)

        nc.vector.memset(xs[:].rearrange("p z t -> p (z t)").bitcast(I32), 0)
        zero_in = sb.tile([P, 1], F32)
        y_wide = sb.tile([P, D, WIDE], F32)
        y_b = sb.tile([P, D, T - 2 * CH - WIDE], F32)
        zero_tile = sb.tile([P, 1], F32)
        zero = zero_tile[:]
        nc.vector.memset(zero_in[:], 0.0)
        nc.vector.memset(y_wide[:, 0, 0:1], 0.0)

        load_whole(raw_h, w3)
        for q in range(4):
            nc.sync.dma_start(
                out=xs[32 * q : 32 * q + 4, :, :].bitcast(I32),
                in_=x_scales[:, 4 * q : 4 * q + 4, :].rearrange("z r t -> r z t").bitcast(I32),
            )
        nc.sync.dma_start(out=xw[:].bitcast(I32), in_=x_words.rearrange("z p b -> p z b").bitcast(I32))
        load_pass(raw_g, w1, 0)
        load_pass(raw_g, w1, 1)
        load_pass(raw_s, w2, 0)
        nc.sync.dma_start(lists[0][:], pos1)
        load_pass(raw_s, w2, 1)
        nc.sync.dma_start(lists[1][:], pos2)
        nc.sync.dma_start(lists[2][:], pos3)

        nc.scalar.activation(out=zero, in_=zero_in[:], func=SILU)
        ident = sb.tile([P, P], F32)
        make_identity(nc, ident[:])

        h_ps = ps.tile([P, T], F32, tag="b0", name="h_ps")
        h2_ps = ps.tile([P, T], F32, tag="b6", name="h2_ps")
        g0_ps = ps.tile([P, T], F32, tag="b1", name="g0_ps")
        gr_ps = ps.tile([P, T], F32, tag="b2", name="gr_ps")
        s0_ps = ps.tile([P, T], F32, tag="b3", name="s0_ps")
        s1_ps = ps.tile([P, T], F32, tag="b7", name="s1_ps")
        sr_ps = ps.tile([P, T], F32, tag="b4", name="sr_ps")

        for z in range(PASSES):
            cast_pass(grp_h[:, z], raw_h[:, z], nc.vector.tensor_copy, 0, SPLIT)
            cast_pass(grp_h[:, z], raw_h[:, z], nc.scalar.copy, SPLIT, M)
        quant("h", 0)
        quant("h", 1)
        mm_chunks("h", (h_ps, h_ps, h2_ps))
        cast_pass(grp_g[0][:], raw_g[0][:], nc.vector.tensor_copy)
        quant("g", 0)
        cast_pass(grp_g[1][:], raw_g[1][:], nc.vector.tensor_copy, 0, SPLIT)
        cast_pass(grp_g[1][:], raw_g[1][:], nc.scalar.copy, SPLIT, M)
        quant("g", 1)
        h_sb = sb.tile([P, T], F32, tag="raw_g1")
        nc.scalar.copy(out=h_sb[:, : T // 2], in_=h_ps[:, : T // 2])
        nc.scalar.copy(out=h_sb[:, T // 2 :], in_=h2_ps[:, T // 2 :])
        mm_chunks("g", (g0_ps, gr_ps))
        cast_pass(grp_s[0][:], raw_s[0][:], nc.vector.tensor_copy)
        quant("s", 0)
        g0_sb = sb.tile([P, CH], F32)
        nc.scalar.copy(out=g0_sb[:], in_=g0_ps[:, :CH])
        cast_pass(grp_s[1][:], raw_s[1][:], nc.scalar.copy)
        gr_sb = sb.tile([P, T - CH], F32, tag="raw_s1")
        nc.scalar.copy(out=gr_sb[:], in_=gr_ps[:, CH:])

        def gather(dst, d, c0, c1):
            nc.vector.tensor_tensor(
                dst,
                h_sb[:].indirect(lists[d][:, c0 // 16 : c1 // 16]),
                g0_sb[:] if c0 == 0 else gr_sb[:, c0 - CH : c1 - CH],
                MULT,
            )

        t = {}

        def gather_block(c, d, tag=""):
            t[c, d] = sb.tile([P, CH], F32, name=f"t{c}_{d}", tag=tag, align_bytes=64)
            gather(t[c, d][:], d, c * CH, (c + 1) * CH)

        gather_block(0, 0, "grp_s0")
        gather_block(0, 1)
        gather_block(0, 2)
        quant("s", 1)
        mm_chunks("s", (s0_ps, s1_ps, sr_ps))
        s0_sb = sb.tile([P, CH], F32)
        sr_sb = sb.tile([P, CH], F32)
        nc.scalar.copy(out=s0_sb[:], in_=s0_ps[:, :CH])
        nc.scalar.copy(out=sr_sb[:], in_=s1_ps[:, CH : 2 * CH])

        def xpose(dst, src, start, stop):
            nc.tensor.matmul(dst, lhsT=src, rhs=ident[:], start=start, stop=stop, is_transpose=True)

        u_tags = ("b5", "b1")
        o_tags = ("b0", "b6")
        y = {}

        def forward(c):
            u_ps = ps.tile([P, T], F32, tag=u_tags[c], name=f"u_ps{c}")
            s_c = s0_sb[:] if c == 0 else sr_sb[:]
            for d in range(D):
                dst = u_ps[:, d * P : (d + 1) * P]
                xpose(dst, s_c, True, False)
                xpose(dst, t[c, d][:], False, True)
            y[c] = sb.tile([P, D * P], F32, name=f"y{c}", tag=f"y{c}")
            nc.scalar.activation(out=y[c][:], in_=u_ps[:, : D * P], func=SILU, bias=zero if c == 0 else y_wide[:, 0, 0:1])

        def back(c, copy):
            o_ps = ps.tile([P, T], F32, tag=o_tags[c], name=f"o_ps{c}")
            for d in range(D):
                xpose(o_ps[:, :CH], y[c][:, d * P : (d + 1) * P], d == 0, d == D - 1)
            o_sb = sb.tile([P, CH], F32, name=f"o_sb{c}")
            copy(out=o_sb[:], in_=o_ps[:, :CH])
            nc.sync.dma_start(out=out[:, c * CH : (c + 1) * CH], in_=o_sb[:])

        forward(0)
        for d in range(D):
            gather_block(1, d, ("grp_s1", "", "t_late")[d])
        forward(1)
        back(0, nc.scalar.copy)

        a0, b0 = 2 * CH, 2 * CH + WIDE
        nb = T - b0
        t_a = sb.tile([P, D, WIDE], F32, tag="t_a")
        u_a = sb.tile([P, D, WIDE], F32)
        for d in range(D):
            gather(t_a[:, d, :], d, a0, b0)
        t_b = sb.tile([P, D - 1, nb], F32, tag="t_b")
        for d in range(D - 1):
            gather(t_b[:, d, :], d, b0, T)
        nc.vector.tensor_tensor(u_a[:], t_a[:], sr_ps[:, a0:b0].unsqueeze(1).to_broadcast([P, D, WIDE]), ADD)
        nc.scalar.activation(out=y_wide[:], in_=u_a[:], func=SILU, bias=zero)

        t_last = sb.tile([P, nb], F32, tag="t_late", align_bytes=64)
        gather(t_last[:], D - 1, b0, T)
        u_b = sb.tile([P, D, nb], F32, tag="y0")
        nc.vector.tensor_tensor(u_b[:, : D - 1], t_b[:], sr_ps[:, b0:].unsqueeze(1).to_broadcast([P, D - 1, nb]), ADD)
        nc.scalar.activation(out=y_b[:, : D - 1, :], in_=u_b[:, : D - 1], func=SILU, bias=zero)
        nc.vector.tensor_tensor(u_b[:, D - 1], t_last[:], sr_ps[:, b0:], ADD)
        nc.scalar.activation(out=y_b[:, D - 1, :], in_=u_b[:, D - 1], func=SILU, bias=zero)

        part = sb.tile([P, T - a0], F32)
        o_a = u_b[:, : D - 1].rearrange("p d n -> p (d n)")[:, :WIDE]
        o_b = sb.tile([P, nb], F32)
        nc.vector.tensor_tensor(part[:, :WIDE], y_wide[:, 0, :], y_wide[:, 1, :], ADD)
        nc.vector.tensor_tensor(part[:, WIDE:], y_b[:, 0, :], y_b[:, 1, :], ADD)
        nc.vector.tensor_tensor(o_a[:], part[:, :WIDE], y_wide[:, 2, :], ADD)
        nc.sync.dma_start(out=out[:, a0:b0], in_=o_a[:])
        nc.vector.tensor_tensor(o_b[:], part[:, WIDE:], y_b[:, 2, :], ADD)
        nc.sync.dma_start(out=out[:, b0:], in_=o_b[:])
        back(1, nc.scalar.copy)
